import numpy as np
import ml_dtypes


def mxq(x, axis, fmt="e4m3"):
    dtype, down = {"e4m3": (ml_dtypes.float8_e4m3fn, 7), "e5m2": (ml_dtypes.float8_e5m2, 14)}[fmt]
    v = np.moveaxis(np.asarray(x, np.float32).astype(ml_dtypes.bfloat16).astype(np.float64), axis, -1)
    blocks = v.reshape(v.shape[:-1] + (-1, 32))
    amax = np.abs(blocks).max(-1, keepdims=True)
    byte = np.maximum(np.where(amax > 0, np.frexp(amax)[1] - 1 + 127, 0) - down, 1)
    scale = np.exp2(byte - 127.0)
    codes = (blocks / scale).astype(np.float32).astype(dtype).astype(np.float64)
    return np.moveaxis((codes * scale).reshape(v.shape), -1, axis)


WIDE = False


def mx_kscale(k):
    if not WIDE:
        return np.ones(k)
    levels = np.array([10, -10, 5, -5, 0])
    if k % 512:
        return np.exp2(np.random.permutation(np.resize(levels, k // 32))).repeat(32)
    a = np.empty((k // 512, 16))
    for p in range(k // 512):
        a[p, :8] = np.random.permutation(np.resize(levels, 8))
        for g in range(8):
            far = levels[np.abs(levels - a[p, g]) >= 10]
            a[p, g + 8] = far[np.random.randint(len(far))]
    return np.exp2(a.ravel()).repeat(32)


def f64(x):
    return np.asarray(x).astype(np.float64)


def striped(idx):
    return np.tile(idx.reshape(-1, 16).T, (8, 1)).astype(np.uint16)


def unstriped(offs):
    return offs[:16].T.reshape(-1).astype(np.int64)


def pack_weight(w):
    k, n = w.shape
    w = f64(np.asarray(w, np.float32).astype(ml_dtypes.bfloat16)).reshape(k // 32, 32, n)
    amax = np.abs(w).max(1)
    byte = np.clip(np.where(amax > 0, np.frexp(amax)[1] - 1 + 127 - 7, 1), 1, 254)
    scaled = (w * np.exp2(127.0 - byte)[:, None, :]).reshape(k, n).astype(np.float32)
    words = np.ascontiguousarray(scaled.reshape(k // 512, 128, 4, n).transpose(0, 1, 3, 2)).astype(ml_dtypes.float8_e4m3fn).view(np.uint8)
    return words, np.ascontiguousarray(byte.astype(np.uint8).reshape(k // 512, 16, n))


def unpack_weight(words, scales):
    g, p, n, _ = words.shape
    vals = np.ascontiguousarray(words).view(ml_dtypes.float8_e4m3fn).astype(np.float64) * np.repeat(np.exp2(scales.astype(np.float64) - 127.0), 8, axis=1)[..., None]
    return vals.transpose(0, 1, 3, 2).reshape(g * 512, n)


def sigmoid(v):
    return 1.0 / (1.0 + np.exp(-np.maximum(v, -700.0)))


K, T, S, N, H, W, C = 512, 2048, 512, 512, 512, 2048, 512


def setup_inputs():
    n = np.random.standard_normal
    s = mx_kscale(K)[:, None]
    u = mx_kscale(S)
    packed_xT = pack_weight(n((K, T)) * s)
    return {
        "x_words": packed_xT[0],
        "x_scales": packed_xT[1],
        "w1": (n((K, H)) / np.sqrt(K) / s).astype(np.float32),
        "gn": (np.random.uniform(0.5, 1.5, (H, 1)) * u[:, None]).astype(np.float32),
        "w2": (n((H, N)) / np.sqrt(H) / u[:, None]).astype(np.float32),
        "gs": (np.random.uniform(0.5, 1.5, (K, 1)) / s).astype(np.float32),
        "offs": striped(np.random.permutation(T)[:S]),
        "n1": striped(np.random.randint(0, S, W)),
        "n2": striped(np.random.permutation(S)),
        "cand": striped(np.random.permutation(T)[:C]),
        "n3": striped(np.random.permutation(S)),
        "n4": striped(np.random.permutation(S)),
    }


def reference(x_words, x_scales, w1, gn, w2, gs, offs, n1, n2, cand, n3, n4):
    xq = unpack_weight(x_words, x_scales)[:, unstriped(offs)]
    y = mxq(f64(w1), 0, "e4m3").T @ xq
    mb = y[:, unstriped(n1)]
    sq = (mb) ** 2
    qs = sq.reshape(H, S, 4).sum(axis=2)
    z = f64(gn) * (y / np.sqrt(qs + 0.5))
    a = mxq(f64(w2), 0, "e4m3").T @ mxq(z, 0, "e4m3")
    x_cand = unpack_weight(x_words, x_scales)[:, unstriped(cand)]
    z2 = f64(gs) * (np.maximum(y, y[:, unstriped(n2)]))
    b = 0.0625 * ((x_cand.T @ mxq(z2, 0, "e4m3")))
    return a + (sigmoid(b[:, unstriped(n4)] - b)) * (a[:, unstriped(n3)] - a)

@@ -1,0 +1,294 @@
+from contextlib import ExitStack
+
+import concourse.mybir as mybir
+from concourse.masks import make_identity
+
+F32 = mybir.dt.float32
+BF16 = mybir.dt.bfloat16
+I32 = mybir.dt.int32
+U32 = mybir.dt.uint32
+U16 = mybir.dt.uint16
+U8 = mybir.dt.uint8
+FP8X4 = mybir.dt.float8_e4m3fn_x4
+ALU = mybir.AluOpType
+ACT = mybir.ActivationFunctionType
+
+P = 128
+PACK = 4
+K = 512
+T = 2048
+S = 512
+MEMBERS = 4
+BLOCK = 128
+WIDE = 1024
+NARROW = 528
+MIDDLE = 704
+ON_VECTOR = ((2, 2), (2, 3), (3, 1), (3, 2), (3, 3))
+FLOPS = 3 * 2 * 512 * 512 * 512
+
+
+def tile_picked_fkcdpullbgvarbig_none_p_kernel(tc, x_words, x_scales, w1, gn, w2, gs, offs, n1, n2, cand, n3, n4, out):
+    nc = tc.nc
+    with ExitStack() as ctx:
+        held = ctx.enter_context(tc.tile_pool(name="held", bufs=1))
+        ring = ctx.enter_context(tc.tile_pool(name="ring", bufs=2))
+        psum = ctx.enter_context(tc.psum_pool(name="psum", bufs=2))
+
+        def load_list(name, dram):
+            tile = held.tile(list(dram.shape), U16, name=name)
+            nc.sync.dma_start(tile[:], dram)
+            return tile
+
+        def window(name, width):
+            tile = held.tile([P, width], F32, name=name)
+            nc.gpsimd.memset(tile[:, S:width], 0.0)
+            return tile
+
+        xs = held.tile([P, T], U8, name="xs", align_bytes=64)
+        nc.vector.memset(xs[:].bitcast(I32), 0)
+        offs_t = load_list("offs_t", offs)
+        cand_t = load_list("cand_t", cand)
+        w1_rows = w1.rearrange("(p j) c -> p j c", j=PACK)
+        w1_raw = [held.tile([P, PACK, 256], F32, name="w1_raw%d" % h) for h in range(2)]
+        nc.sync.dma_start(w1_raw[0][:], w1_rows[:, :, 0:256])
+        for q in range(4):
+            nc.sync.dma_start(xs[32 * q : 32 * q + 4, :].bitcast(I32), x_scales[0, 4 * q : 4 * q + 4, :].bitcast(I32))
+        xw = held.tile([P, T], U32, name="xw", align_bytes=64)
+        nc.sync.dma_start(xw[:].bitcast(I32), x_words[0].rearrange("p n t -> p (n t)").bitcast(I32))
+        nc.sync.dma_start(w1_raw[1][:], w1_rows[:, :, 256:512])
+        n1_t = load_list("n1_t", n1)
+        n2_t = load_list("n2_t", n2)
+        gn_t = held.tile([P, PACK], F32, name="gn_t")
+        gs_t = held.tile([P, PACK], F32, name="gs_t")
+        nc.sync.dma_start(gn_t[:], gn.rearrange("(p t) o -> p (t o)", t=PACK))
+        nc.sync.dma_start(gs_t[:], gs.rearrange("(p t) o -> p (t o)", t=PACK))
+        w2_raw = held.tile([P, PACK, 512], F32, name="w2_raw")
+        nc.sync.dma_start(w2_raw[:], w2.rearrange("(p j) c -> p j c", j=PACK))
+        n4_t = load_list("n4_t", n4)
+        n3_t = load_list("n3_t", n3)
+
+        ident = held.tile([P, P], F32, name="ident")
+        make_identity(nc, ident[:])
+        sq = [window("sq%d" % t, WIDE) for t in range(PACK)]
+        y = [window("y%d" % t, MIDDLE) for t in range(PACK)]
+        a_win = [window("a_win%d" % t, MIDDLE) for t in range(PACK)]
+        b_win = [window("b_win%d" % t, MIDDLE) for t in range(PACK)]
+
+        xq_s = held.tile([P, S], U8, name="xq_s", align_bytes=64)
+        xq_w = held.tile([P, S], U32, name="xq_w", align_bytes=64)
+        xc_s = held.tile([P, S], U8, name="xc_s", align_bytes=64)
+        xc_w = held.tile([P, S], U32, name="xc_w", align_bytes=64)
+        nc.vector.tensor_copy(xq_s[:], xs[:].indirect(offs_t[:]))
+        nc.vector.tensor_copy(xc_s[:], xs[:].indirect(cand_t[:]))
+        nc.vector.tensor_copy(xq_w[:], xw[:].indirect(offs_t[:]))
+        nc.vector.tensor_copy(xc_w[:], xw[:].indirect(cand_t[:]))
+
+        w1_bf = held.tile([P, PACK * 512], BF16, name="w1_bf", align_bytes=64)
+        w1_view = w1_bf[:].rearrange("p (t m j) -> p m j t", t=PACK, j=PACK)
+        w1_in = [raw[:].rearrange("p j (m t) -> p m j t", t=PACK) for raw in w1_raw]
+        nc.scalar.copy(w1_view[:, 0:64], w1_in[0])
+        nc.scalar.copy(w1_view[:, 64:128], w1_in[1])
+        w1_w = held.tile([P, 512], U32, name="w1_w", align_bytes=64)
+        w1_s = held.tile([P, 512], U8, name="w1_s", align_bytes=64)
+        y_ps = []
+        for t in range(PACK):
+            cols = slice(P * t, P * (t + 1))
+            nc.vector.quantize_mx(out=w1_w[:, cols].bitcast(FP8X4), scales=w1_s[:, cols], in_=w1_bf[:, 512 * t : 512 * (t + 1)])
+            acc = psum.tile([P, S], F32, name="y_ps", tag="acc", bufs=4)
+            nc.tensor.matmul_mx(out=acc[:], lhsT=w1_w[:, cols].bitcast(FP8X4), lhsT_scale=w1_s[:, cols],
+                                rhs=xq_w[:].bitcast(FP8X4), rhs_scale=xq_s[:], start=True, stop=True)
+            y_ps.append(acc)
+
+        yn = held.tile([P, PACK, S], F32, name="yn")
+        for t in range(PACK):
+            nc.scalar.activation(sq[t][:, 0:S], y_ps[t][:], ACT.Square)
+            nc.vector.tensor_copy(y[t][:, 0:S], y_ps[t][:])
+
+        w2_bf = held.tile([P, PACK * 512], BF16, name="w2_bf", align_bytes=64)
+        w2_w = held.tile([P, 512], U32, name="w2_w", align_bytes=64)
+        w2_s = held.tile([P, 512], U8, name="w2_s", align_bytes=64)
+        z_bf = held.tile([P, PACK * S], BF16, name="z_bf", align_bytes=64)
+        z_w = held.tile([P, S], U32, name="z_w", align_bytes=64)
+        z_s = held.tile([P, S], U8, name="z_s", align_bytes=64)
+        top = ring.tile([P, PACK, S], F32, name="top", tag="planes", bufs=1)
+        z2_bf = held.tile([P, PACK * S], BF16, name="z2_bf", align_bytes=64)
+        z2_w = held.tile([P, S], U32, name="z2_w", align_bytes=64)
+        z2_s = held.tile([P, S], U8, name="z2_s", align_bytes=64)
+
+        def gain(t):
+            nc.gpsimd.tensor_scalar(yn[:, t, :], y[t][:, 0:S], gn_t[:, t : t + 1], 0.0, ALU.mult, ALU.add)
+
+        def round_w2():
+            nc.gpsimd.tensor_copy(w2_bf[:].rearrange("p (c j) -> p c j", j=PACK), w2_raw[:].rearrange("p j c -> p c j"))
+
+        def quantise_w2():
+            nc.vector.quantize_mx(out=w2_w[:].bitcast(FP8X4), scales=w2_s[:], in_=w2_bf[:])
+
+        sums = {}
+        late = []
+
+        def members(b, t):
+            offsets = n1_t[:, 32 * b : 32 * (b + 1)]
+            if t == 0:
+                sums[b] = psum.tile([P, PACK, P], F32, name="sums", tag="sums")
+            if (b, t) in ON_VECTOR:
+                if not late:
+                    late.append(ring.tile([P, len(ON_VECTOR), MEMBERS, BLOCK], F32, name="late", tag="planes", bufs=1))
+                member = late[0][:, ON_VECTOR.index((b, t)), :, :]
+                nc.vector.tensor_copy(member.rearrange("p u j -> p j u"), sq[t][:].indirect(offsets))
+            else:
+                g = ring.tile([P, MEMBERS * BLOCK], F32, name="ga", bufs=4)
+                nc.scalar.activation(g[:], sq[t][:].indirect(offsets), ACT.Copy)
+                member = g[:].rearrange("p (j u) -> p u j", u=MEMBERS)
+            for u in range(MEMBERS):
+                nc.tensor.matmul(sums[b][:, t, :], member[:, u, :], ident[:], start=(u == 0), stop=(u == MEMBERS - 1), is_transpose=True)
+
+        def inverse_root(b):
+            r_t = ring.tile([P, PACK, P], F32, name="r_t")
+            nc.scalar.activation(r_t[:], sums[b][:], ACT.Abs_reciprocal_sqrt, bias=0.5)
+            r = psum.tile([P, PACK, P], F32, name="r", tag="r")
+            for t in range(PACK):
+                nc.tensor.transpose(r[:, t, :], r_t[:, t, :], ident[:])
+            return r
+
+        def make_z(b, r):
+            cols = slice(BLOCK * b, BLOCK * (b + 1))
+            wide = slice(PACK * BLOCK * b, PACK * BLOCK * (b + 1))
+            nc.vector.tensor_tensor(z_bf[:, wide].rearrange("p (c i t) -> p c t i", i=4, t=PACK),
+                                    r[:].rearrange("p t (c i) -> p c t i", i=4),
+                                    yn[:, :, cols].rearrange("p t (c i) -> p c t i", i=4), ALU.mult)
+
+        def quantise_z(b):
+            cols = slice(BLOCK * b, BLOCK * (b + 1))
+            wide = slice(PACK * BLOCK * b, PACK * BLOCK * (b + 1))
+            nc.vector.quantize_mx(out=z_w[:, cols].bitcast(FP8X4), scales=z_s[:, cols], in_=z_bf[:, wide])
+
+        def larger(t):
+            return fetch("v", "yg", y[t], n2_t)
+
+        def weigh(t, yg):
+            nc.vector.tensor_tensor(top[:, t, :], yg[:], y[t][:, 0:S], ALU.max)
+
+        def weave_z2():
+            nc.vector.tensor_tensor(z2_bf[:].rearrange("p (c i t) -> p c t i", i=4, t=PACK),
+                                    top[:].rearrange("p t (c i) -> p c t i", i=4),
+                                    gs_t[:].unsqueeze(1).unsqueeze(3).to_broadcast([P, S // 4, PACK, 4]), ALU.mult)
+
+        def quantise_z2():
+            nc.vector.quantize_mx(out=z2_w[:].bitcast(FP8X4), scales=z2_s[:], in_=z2_bf[:])
+
+        def product_b(m):
+            cols = slice(P * m, P * (m + 1))
+            acc = psum.tile([P, S], F32, name="b_ps", tag="acc", bufs=4)
+            nc.tensor.matmul_mx(out=acc[:], lhsT=xc_w[:, cols].bitcast(FP8X4), lhsT_scale=xc_s[:, cols],
+                                rhs=z2_w[:].bitcast(FP8X4), rhs_scale=z2_s[:], start=True, stop=True)
+            return acc
+
+        def product_a(m):
+            cols = slice(P * m, P * (m + 1))
+            acc = psum.tile([P, S], F32, name="a_ps", tag=("sums", "r")[m % 2])
+            nc.tensor.matmul_mx(out=acc[:], lhsT=w2_w[:, cols].bitcast(FP8X4), lhsT_scale=w2_s[:, cols],
+                                rhs=z_w[:].bitcast(FP8X4), rhs_scale=z_s[:], start=True, stop=True)
+            return acc
+
+        def evac(eng, win, ps):
+            if eng == "v":
+                nc.vector.tensor_copy(win[:, 0:S], ps[:])
+            else:
+                nc.scalar.copy(win[:, 0:S], ps[:])
+
+        def fetch(eng, name, win, offsets):
+            got = ring.tile([P, S], F32, name=name, bufs=4)
+            if eng == "v":
+                nc.vector.tensor_copy(got[:], win[:].indirect(offsets[:]))
+            else:
+                nc.scalar.activation(got[:], win[:].indirect(offsets[:]), ACT.Copy)
+            return got
+
+        def gate_of(m, bg):
+            db = ring.tile([P, S], F32, name="db", bufs=4)
+            nc.vector.tensor_tensor(db[:], bg[:], b_ps[m][:], ALU.subtract)
+            return db
+
+        def squash(db):
+            gate = ring.tile([P, S], F32, name="gate", bufs=4)
+            nc.scalar.activation(gate[:], db[:], ACT.Sigmoid, scale=0.0625)
+            return gate
+
+        def kept(m, gate):
+            keep = ring.tile([P, S], F32, name="keep", bufs=4)
+            nc.vector.scalar_tensor_tensor(keep[:], gate[:], 1.0, a_ps[m][:], ALU.subtract, ALU.mult)
+            return keep
+
+        def pulled(m, ag, gate):
+            pull = ring.tile([P, S], F32, name="pull")
+            nc.vector.tensor_tensor(pull[:], ag[:], gate[:], ALU.mult)
+            return pull
+
+        def store(m, pull, keep):
+            res = ring.tile([P, S], F32, name="res")
+            nc.vector.tensor_tensor(res[:], pull[:], keep[:], ALU.subtract)
+            nc.sync.dma_start(out[P * m : P * (m + 1), :], res[:])
+
+        for t in range(4):
+            members(0, t)
+        yg = larger(0)
+        for t in range(4):
+            now = yg
+            if t < 3:
+                yg = larger(t + 1)
+            weigh(t, now)
+            gain(t)
+        round_w2()
+        members(1, 0)
+        r0 = inverse_root(0)
+        for t in range(1, 4):
+            members(1, t)
+        weave_z2()
+        make_z(0, r0)
+        quantise_z2()
+        quantise_z(0)
+        b_ps = [product_b(m) for m in range(4)]
+        members(2, 0)
+        r1 = inverse_root(1)
+        for t in range(1, 4):
+            members(2, t)
+        make_z(1, r1)
+        members(3, 0)
+        members(3, 1)
+        quantise_z(1)
+        members(3, 2)
+        members(3, 3)
+        bg = []
+        evac("s", b_win[0], b_ps[0])
+        bg.append(fetch("s", "bg", b_win[0], n4_t))
+        r2 = inverse_root(2)
+        make_z(2, r2)
+        quantise_w2()
+        quantise_z(2)
+        for m in range(1, 2):
+            evac("s", b_win[m], b_ps[m])
+            bg.append(fetch("s", "bg", b_win[m], n4_t))
+        r3 = inverse_root(3)
+        make_z(3, r3)
+        for m in range(2, 4):
+            evac("s", b_win[m], b_ps[m])
+            bg.append(fetch("s", "bg", b_win[m], n4_t))
+        db = [gate_of(0, bg[0])]
+        quantise_z(3)
+        a_ps = [product_a(m) for m in range(4)]
+        db.append(gate_of(1, bg[1]))
+        db.append(gate_of(2, bg[2]))
+        db.append(gate_of(3, bg[3]))
+        gate = [squash(db[0])]
+        pull = None
+        for m in range(4):
+            evac("vvss"[m], a_win[m], a_ps[m])
+            keep = kept(m, gate[m])
+            if m < 3:
+                gate.append(squash(db[m + 1]))
+            ag = fetch("ssss"[m], "ag", a_win[m], n3_t)
+            if pull is not None:
+                store(m - 1, *pull)
+            pull = (pulled(m, ag, gate[m]), keep)
+        store(3, *pull)

@@ -15,15 +15,13 @@ ACT = mybir.ActivationFunctionType
 
 P = 128
 PACK = 4
-K = 512
 T = 2048
 S = 512
 MEMBERS = 4
 BLOCK = 128
-WIDE = 1024
-NARROW = 528
-MIDDLE = 704
-ON_VECTOR = ((2, 2), (2, 3), (3, 1), (3, 2), (3, 3))
+SQUARES_WIDTH = 1024
+SCORES_WIDTH = 528
+ON_SCALAR = ((1, 2), (1, 3), (2, 2), (2, 3))
 FLOPS = 3 * 2 * 512 * 512 * 512
 
 
@@ -39,9 +37,9 @@ def tile_picked_fkcdpullbgvarbig_none_p_kernel(tc, x_words, x_scales, w1, gn, w2
             nc.sync.dma_start(tile[:], dram)
             return tile
 
-        def window(name, width):
+        def window(name, live, width):
             tile = held.tile([P, width], F32, name=name)
-            nc.gpsimd.memset(tile[:, S:width], 0.0)
+            nc.gpsimd.memset(tile[:, live:width], 0.0)
             return tile
 
         xs = held.tile([P, T], U8, name="xs", align_bytes=64)
@@ -53,41 +51,40 @@ def tile_picked_fkcdpullbgvarbig_none_p_kernel(tc, x_words, x_scales, w1, gn, w2
         nc.sync.dma_start(w1_raw[0][:], w1_rows[:, :, 0:256])
         for q in range(4):
             nc.sync.dma_start(xs[32 * q : 32 * q + 4, :].bitcast(I32), x_scales[0, 4 * q : 4 * q + 4, :].bitcast(I32))
-        xw = held.tile([P, T], U32, name="xw", align_bytes=64)
+        xw = held.tile([P, T], U32, name="xw", tag="table", align_bytes=64)
         nc.sync.dma_start(xw[:].bitcast(I32), x_words[0].rearrange("p n t -> p (n t)").bitcast(I32))
         nc.sync.dma_start(w1_raw[1][:], w1_rows[:, :, 256:512])
         n1_t = load_list("n1_t", n1)
-        n2_t = load_list("n2_t", n2)
-        gn_t = held.tile([P, PACK], F32, name="gn_t")
         gs_t = held.tile([P, PACK], F32, name="gs_t")
-        nc.sync.dma_start(gn_t[:], gn.rearrange("(p t) o -> p (t o)", t=PACK))
+        gn_t = held.tile([P, PACK], F32, name="gn_t")
         nc.sync.dma_start(gs_t[:], gs.rearrange("(p t) o -> p (t o)", t=PACK))
-        w2_raw = held.tile([P, PACK, 512], F32, name="w2_raw")
-        nc.sync.dma_start(w2_raw[:], w2.rearrange("(p j) c -> p j c", j=PACK))
+        n2_t = load_list("n2_t", n2)
+        nc.sync.dma_start(gn_t[:], gn.rearrange("(p t) o -> p (t o)", t=PACK))
         n4_t = load_list("n4_t", n4)
         n3_t = load_list("n3_t", n3)
 
         ident = held.tile([P, P], F32, name="ident")
         make_identity(nc, ident[:])
-        sq = [window("sq%d" % t, WIDE) for t in range(PACK)]
-        y = [window("y%d" % t, MIDDLE) for t in range(PACK)]
-        a_win = [window("a_win%d" % t, MIDDLE) for t in range(PACK)]
-        b_win = [window("b_win%d" % t, MIDDLE) for t in range(PACK)]
+        warm = held.tile([P, 1], F32, name="warm")
+        nc.scalar.activation(warm[:], ident[:, 0:1], ACT.Abs_reciprocal_sqrt, bias=0.5)
+        sq = [window("sq%d" % t, S, SQUARES_WIDTH) for t in range(PACK)]
+        y_abs = window("y_abs", PACK * S, (PACK + 1) * S)
+        a_all = window("a_all", PACK * S, (PACK + 1) * S)
+        b_win = [window("b_win%d" % t, S, SCORES_WIDTH) for t in range(PACK)]
 
         xq_s = held.tile([P, S], U8, name="xq_s", align_bytes=64)
         xq_w = held.tile([P, S], U32, name="xq_w", align_bytes=64)
         xc_s = held.tile([P, S], U8, name="xc_s", align_bytes=64)
-        xc_w = held.tile([P, S], U32, name="xc_w", align_bytes=64)
         nc.vector.tensor_copy(xq_s[:], xs[:].indirect(offs_t[:]))
         nc.vector.tensor_copy(xc_s[:], xs[:].indirect(cand_t[:]))
         nc.vector.tensor_copy(xq_w[:], xw[:].indirect(offs_t[:]))
-        nc.vector.tensor_copy(xc_w[:], xw[:].indirect(cand_t[:]))
 
-        w1_bf = held.tile([P, PACK * 512], BF16, name="w1_bf", align_bytes=64)
+        w1_bf = held.tile([P, PACK * 512], BF16, name="w1_bf", tag="rounded", align_bytes=64)
         w1_view = w1_bf[:].rearrange("p (t m j) -> p m j t", t=PACK, j=PACK)
         w1_in = [raw[:].rearrange("p j (m t) -> p m j t", t=PACK) for raw in w1_raw]
         nc.scalar.copy(w1_view[:, 0:64], w1_in[0])
-        nc.scalar.copy(w1_view[:, 64:128], w1_in[1])
+        nc.scalar.copy(w1_view[:, 64:96], w1_in[1][:, 0:32])
+        nc.vector.tensor_copy(w1_view[:, 96:128], w1_in[1][:, 32:64])
         w1_w = held.tile([P, 512], U32, name="w1_w", align_bytes=64)
         w1_s = held.tile([P, 512], U8, name="w1_s", align_bytes=64)
         y_ps = []
@@ -98,54 +95,53 @@ def tile_picked_fkcdpullbgvarbig_none_p_kernel(tc, x_words, x_scales, w1, gn, w2
             nc.tensor.matmul_mx(out=acc[:], lhsT=w1_w[:, cols].bitcast(FP8X4), lhsT_scale=w1_s[:, cols],
                                 rhs=xq_w[:].bitcast(FP8X4), rhs_scale=xq_s[:], start=True, stop=True)
             y_ps.append(acc)
+        xc_w = held.tile([P, S], U32, name="xc_w", tag="rounded", align_bytes=64)
+        nc.vector.tensor_copy(xc_w[:], xw[:].indirect(cand_t[:]))
+        w2_raw = held.tile([P, PACK, 512], F32, name="w2_raw", tag="table", align_bytes=64)
+        nc.sync.dma_start(w2_raw[:], w2.rearrange("(p j) c -> p j c", j=PACK))
 
-        yn = held.tile([P, PACK, S], F32, name="yn")
+        gs_abs = held.tile([P, PACK], F32, name="gs_abs")
+        nc.scalar.activation(gs_abs[:], gs_t[:], ACT.Abs)
+        gs_sign = held.tile([P, BLOCK, PACK], BF16, name="gs_sign")
+        nc.scalar.activation(gs_sign[:], gs_t[:].unsqueeze(1).to_broadcast([P, BLOCK, PACK]), ACT.Sign)
+
         for t in range(PACK):
             nc.scalar.activation(sq[t][:, 0:S], y_ps[t][:], ACT.Square)
-            nc.vector.tensor_copy(y[t][:, 0:S], y_ps[t][:])
 
+        yn = held.tile([P, PACK, S], F32, name="yn")
+        yg = held.tile([P, PACK, S], F32, name="yg")
         w2_bf = held.tile([P, PACK * 512], BF16, name="w2_bf", align_bytes=64)
         w2_w = held.tile([P, 512], U32, name="w2_w", align_bytes=64)
         w2_s = held.tile([P, 512], U8, name="w2_s", align_bytes=64)
-        z_bf = held.tile([P, PACK * S], BF16, name="z_bf", align_bytes=64)
         z_w = held.tile([P, S], U32, name="z_w", align_bytes=64)
         z_s = held.tile([P, S], U8, name="z_s", align_bytes=64)
-        top = ring.tile([P, PACK, S], F32, name="top", tag="planes", bufs=1)
-        z2_bf = held.tile([P, PACK * S], BF16, name="z2_bf", align_bytes=64)
+        top_bf = held.tile([P, PACK * S], BF16, name="top_bf", tag="planes", align_bytes=64)
+        z2_bf = held.tile([P, PACK * S], BF16, name="z2_bf", tag="woven", align_bytes=64)
         z2_w = held.tile([P, S], U32, name="z2_w", align_bytes=64)
         z2_s = held.tile([P, S], U8, name="z2_s", align_bytes=64)
-
-        def gain(t):
-            nc.gpsimd.tensor_scalar(yn[:, t, :], y[t][:, 0:S], gn_t[:, t : t + 1], 0.0, ALU.mult, ALU.add)
-
-        def round_w2():
-            nc.gpsimd.tensor_copy(w2_bf[:].rearrange("p (c j) -> p c j", j=PACK), w2_raw[:].rearrange("p j c -> p c j"))
-
-        def quantise_w2():
-            nc.vector.quantize_mx(out=w2_w[:].bitcast(FP8X4), scales=w2_s[:], in_=w2_bf[:])
-
+        db = held.tile([P, PACK, S], F32, name="db")
         sums = {}
-        late = []
 
-        def members(b, t):
+        def members(b, t, g):
             offsets = n1_t[:, 32 * b : 32 * (b + 1)]
-            if t == 0:
+            if b not in sums:
                 sums[b] = psum.tile([P, PACK, P], F32, name="sums", tag="sums")
-            if (b, t) in ON_VECTOR:
-                if not late:
-                    late.append(ring.tile([P, len(ON_VECTOR), MEMBERS, BLOCK], F32, name="late", tag="planes", bufs=1))
-                member = late[0][:, ON_VECTOR.index((b, t)), :, :]
-                nc.vector.tensor_copy(member.rearrange("p u j -> p j u"), sq[t][:].indirect(offsets))
+            if (b, t) in ON_SCALAR:
+                nc.scalar.activation(g, sq[t][:].indirect(offsets), ACT.Copy)
+                member = g.rearrange("p (j u) -> p u j", u=MEMBERS)
             else:
-                g = ring.tile([P, MEMBERS * BLOCK], F32, name="ga", bufs=4)
-                nc.scalar.activation(g[:], sq[t][:].indirect(offsets), ACT.Copy)
-                member = g[:].rearrange("p (j u) -> p u j", u=MEMBERS)
+                member = g.rearrange("p (u j) -> p u j", u=MEMBERS)
+                nc.vector.tensor_copy(member.rearrange("p u j -> p j u"), sq[t][:].indirect(offsets))
             for u in range(MEMBERS):
                 nc.tensor.matmul(sums[b][:, t, :], member[:, u, :], ident[:], start=(u == 0), stop=(u == MEMBERS - 1), is_transpose=True)
 
-        def inverse_root(b):
-            r_t = ring.tile([P, PACK, P], F32, name="r_t")
-            nc.scalar.activation(r_t[:], sums[b][:], ACT.Abs_reciprocal_sqrt, bias=0.5)
+        def early_members(b, t):
+            g = ring.tile([P, MEMBERS * BLOCK], F32, name="early", bufs=8)
+            members(b, t, g[:])
+
+        def inverse_root(b, r_flat):
+            r_t = r_flat.rearrange("p (t i) -> p t i", t=PACK)
+            nc.scalar.activation(r_t, sums[b][:], ACT.Abs_reciprocal_sqrt, bias=0.5)
             r = psum.tile([P, PACK, P], F32, name="r", tag="r")
             for t in range(PACK):
                 nc.tensor.transpose(r[:, t, :], r_t[:, t, :], ident[:])
@@ -163,19 +159,17 @@ def tile_picked_fkcdpullbgvarbig_none_p_kernel(tc, x_words, x_scales, w1, gn, w2
             wide = slice(PACK * BLOCK * b, PACK * BLOCK * (b + 1))
             nc.vector.quantize_mx(out=z_w[:, cols].bitcast(FP8X4), scales=z_s[:, cols], in_=z_bf[:, wide])
 
-        def larger(t):
-            return fetch("v", "yg", y[t], n2_t)
+        def evac(eng, to, ps):
+            if eng == "v":
+                nc.vector.tensor_copy(to, ps)
+            else:
+                nc.scalar.copy(to, ps)
 
-        def weigh(t, yg):
-            nc.vector.tensor_tensor(top[:, t, :], yg[:], y[t][:, 0:S], ALU.max)
-
-        def weave_z2():
-            nc.vector.tensor_tensor(z2_bf[:].rearrange("p (c i t) -> p c t i", i=4, t=PACK),
-                                    top[:].rearrange("p t (c i) -> p c t i", i=4),
-                                    gs_t[:].unsqueeze(1).unsqueeze(3).to_broadcast([P, S // 4, PACK, 4]), ALU.mult)
-
-        def quantise_z2():
-            nc.vector.quantize_mx(out=z2_w[:].bitcast(FP8X4), scales=z2_s[:], in_=z2_bf[:])
+        def fetch(eng, got, win, offsets):
+            if eng == "v":
+                nc.vector.tensor_copy(got, win.indirect(offsets))
+            else:
+                nc.scalar.activation(got, win.indirect(offsets), ACT.Copy)
 
         def product_b(m):
             cols = slice(P * m, P * (m + 1))
@@ -184,111 +178,124 @@ def tile_picked_fkcdpullbgvarbig_none_p_kernel(tc, x_words, x_scales, w1, gn, w2
                                 rhs=z2_w[:].bitcast(FP8X4), rhs_scale=z2_s[:], start=True, stop=True)
             return acc
 
-        def product_a(m):
-            cols = slice(P * m, P * (m + 1))
-            acc = psum.tile([P, S], F32, name="a_ps", tag=("sums", "r")[m % 2])
-            nc.tensor.matmul_mx(out=acc[:], lhsT=w2_w[:, cols].bitcast(FP8X4), lhsT_scale=w2_s[:, cols],
-                                rhs=z_w[:].bitcast(FP8X4), rhs_scale=z_s[:], start=True, stop=True)
-            return acc
+        def product_a(b):
+            cols = slice(BLOCK * b, BLOCK * (b + 1))
+            acc = psum.tile([P, PACK, BLOCK], F32, name="a_ps", tag="sums") if b < 2 else psum.tile([P, PACK, BLOCK], F32, name="a_ps", tag="acc", bufs=4)
+            for m in range(PACK):
+                rows = slice(P * m, P * (m + 1))
+                nc.tensor.matmul_mx(out=acc[:, m, :], lhsT=w2_w[:, rows].bitcast(FP8X4), lhsT_scale=w2_s[:, rows],
+                                    rhs=z_w[:, cols].bitcast(FP8X4), rhs_scale=z_s[:, cols], start=True, stop=True)
+            evac("vvvv"[b], a_all[:, 0 : PACK * S].rearrange("p (m j) -> p m j", m=PACK)[:, :, cols], acc[:])
 
-        def evac(eng, win, ps):
-            if eng == "v":
-                nc.vector.tensor_copy(win[:, 0:S], ps[:])
-            else:
-                nc.scalar.copy(win[:, 0:S], ps[:])
+        bg = [ring.tile([P, S], F32, name="bg%d" % m, bufs=1) for m in range(PACK)]
 
-        def fetch(eng, name, win, offsets):
-            got = ring.tile([P, S], F32, name=name, bufs=4)
-            if eng == "v":
-                nc.vector.tensor_copy(got[:], win[:].indirect(offsets[:]))
-            else:
-                nc.scalar.activation(got[:], win[:].indirect(offsets[:]), ACT.Copy)
-            return got
+        def copy_b(m):
+            nc.scalar.copy(b_win[m][:, 0:S], b_ps[m][:])
 
-        def gate_of(m, bg):
-            db = ring.tile([P, S], F32, name="db", bufs=4)
-            nc.vector.tensor_tensor(db[:], bg[:], b_ps[m][:], ALU.subtract)
-            return db
+        def fetch_b(m):
+            fetch("ssss"[m], bg[m][:], b_win[m][:], n4_t[:])
 
-        def squash(db):
-            gate = ring.tile([P, S], F32, name="gate", bufs=4)
-            nc.scalar.activation(gate[:], db[:], ACT.Sigmoid, scale=0.0625)
-            return gate
+        def differ(m):
+            nc.vector.tensor_tensor(db[:, m, :], bg[m][:], b_win[m][:, 0:S], ALU.subtract)
 
-        def kept(m, gate):
+        def squash(m):
+            nc.scalar.activation(gates[:, m, :], db[:, m, :], ACT.Sigmoid, scale=0.0625)
+
+        def kept(m):
             keep = ring.tile([P, S], F32, name="keep", bufs=4)
-            nc.vector.scalar_tensor_tensor(keep[:], gate[:], 1.0, a_ps[m][:], ALU.subtract, ALU.mult)
+            nc.vector.scalar_tensor_tensor(keep[:], gates[:, m, :], 1.0, a_all[:, S * m : S * (m + 1)], ALU.subtract, ALU.mult)
             return keep
 
-        def pulled(m, ag, gate):
-            pull = ring.tile([P, S], F32, name="pull")
-            nc.vector.tensor_tensor(pull[:], ag[:], gate[:], ALU.mult)
+        def pulled(m, cols, ag):
+            pull = ring.tile([P, cols.stop - cols.start], F32, name="pull", bufs=3)
+            nc.vector.tensor_tensor(pull[:], ag[:], gates[:, m, cols], ALU.mult)
             return pull
 
-        def store(m, pull, keep):
-            res = ring.tile([P, S], F32, name="res")
-            nc.vector.tensor_tensor(res[:], pull[:], keep[:], ALU.subtract)
-            nc.sync.dma_start(out[P * m : P * (m + 1), :], res[:])
+        def store(m, cols, pull, keep):
+            res = ring.tile([P, cols.stop - cols.start], F32, name="res", bufs=5)
+            nc.vector.tensor_tensor(res[:], pull[:], keep[:, cols], ALU.subtract)
+            nc.sync.dma_start(out[P * m : P * (m + 1), cols], res[:])
 
-        for t in range(4):
-            members(0, t)
-        yg = larger(0)
-        for t in range(4):
-            now = yg
-            if t < 3:
-                yg = larger(t + 1)
-            weigh(t, now)
-            gain(t)
-        round_w2()
-        members(1, 0)
-        r0 = inverse_root(0)
-        for t in range(1, 4):
-            members(1, t)
-        weave_z2()
+        for t in range(PACK):
+            early_members(0, t)
+        for t in range(PACK + 1):
+            if t < PACK:
+                nc.scalar.activation(y_abs[:, S * t : S * (t + 1)], y_ps[t][:], ACT.Copy, scale=gs_abs[:, t : t + 1])
+            if t > 0:
+                fetch("s", yg[:, t - 1, :], y_abs[:, S * (t - 1) : S * (t + 1)], n2_t[:])
+        root0 = held.tile([P, S], F32, name="root0")
+        r0 = inverse_root(0, root0[:])
+        nc.vector.tensor_tensor(top_bf[:].rearrange("p (c i t) -> p c t i", i=4, t=PACK),
+                                yg[:].rearrange("p t (c i) -> p c t i", i=4),
+                                y_abs[:, 0 : PACK * S].rearrange("p (t c i) -> p c t i", t=PACK, i=4), ALU.max)
+        for t in range(PACK):
+            early_members(1, t)
+        for t in range(PACK):
+            nc.scalar.activation(yn[:, t, :], y_ps[t][:], ACT.Copy, scale=gn_t[:, t : t + 1])
+        nc.vector.tensor_tensor(z2_bf[:].rearrange("p (b w) -> p b w", b=4), top_bf[:].rearrange("p (b w) -> p b w", b=4),
+                                gs_sign[:].rearrange("p c t -> p (c t)").unsqueeze(1).to_broadcast([P, 4, PACK * BLOCK]), ALU.mult)
+        for h in range(4):
+            cols = slice(P * h, P * (h + 1))
+            nc.vector.tensor_copy(w2_bf[:, PACK * P * h : PACK * P * (h + 1)].rearrange("p (c i j) -> p c j i", i=4, j=PACK),
+                                  w2_raw[:, :, cols].rearrange("p j (c i) -> p c j i", i=4))
+        nc.vector.quantize_mx(out=z2_w[:].bitcast(FP8X4), scales=z2_s[:], in_=z2_bf[:])
+        b_ps = [product_b(m) for m in range(PACK)]
+        z_bf = held.tile([P, PACK * S], BF16, name="z_bf", tag="planes", align_bytes=64)
+        late = held.tile([P, 3, PACK, MEMBERS * BLOCK], F32, name="late", tag="woven", align_bytes=64)
+
+        def late_members(b, t):
+            members(b, t, late[:, b - 2, t, :])
+
+        r1 = inverse_root(1, late[:, 2, 1, :])
+        late_members(2, 2)
+        late_members(2, 3)
         make_z(0, r0)
-        quantise_z2()
+        late_members(2, 0)
         quantise_z(0)
-        b_ps = [product_b(m) for m in range(4)]
-        members(2, 0)
-        r1 = inverse_root(1)
-        for t in range(1, 4):
-            members(2, t)
+        late_members(2, 1)
+        nc.vector.quantize_mx(out=w2_w[:].bitcast(FP8X4), scales=w2_s[:], in_=w2_bf[:])
         make_z(1, r1)
-        members(3, 0)
-        members(3, 1)
+        late_members(3, 0)
         quantise_z(1)
-        members(3, 2)
-        members(3, 3)
-        bg = []
-        evac("s", b_win[0], b_ps[0])
-        bg.append(fetch("s", "bg", b_win[0], n4_t))
-        r2 = inverse_root(2)
+        for t in range(1, PACK):
+            late_members(3, t)
+        copy_b(0)
+        copy_b(1)
+        fetch_b(0)
+        copy_b(2)
+        copy_b(3)
+        fetch_b(1)
+        r2 = inverse_root(2, late[:, 2, 2, :])
+        fetch_b(2)
+        r3 = inverse_root(3, late[:, 2, 3, :])
+        fetch_b(3)
+        differ(0)
         make_z(2, r2)
-        quantise_w2()
+        differ(1)
         quantise_z(2)
-        for m in range(1, 2):
-            evac("s", b_win[m], b_ps[m])
-            bg.append(fetch("s", "bg", b_win[m], n4_t))
-        r3 = inverse_root(3)
         make_z(3, r3)
-        for m in range(2, 4):
-            evac("s", b_win[m], b_ps[m])
-            bg.append(fetch("s", "bg", b_win[m], n4_t))
-        db = [gate_of(0, bg[0])]
+        product_a(0)
         quantise_z(3)
-        a_ps = [product_a(m) for m in range(4)]
-        db.append(gate_of(1, bg[1]))
-        db.append(gate_of(2, bg[2]))
-        db.append(gate_of(3, bg[3]))
-        gate = [squash(db[0])]
-        pull = None
-        for m in range(4):
-            evac("vvss"[m], a_win[m], a_ps[m])
-            keep = kept(m, gate[m])
-            if m < 3:
-                gate.append(squash(db[m + 1]))
-            ag = fetch("ssss"[m], "ag", a_win[m], n3_t)
-            if pull is not None:
-                store(m - 1, *pull)
-            pull = (pulled(m, ag, gate[m]), keep)
-        store(3, *pull)
+        gates = held.tile([P, PACK, S], F32, name="gates", tag="woven", align_bytes=64)
+        squash(0)
+        for b in range(1, 4):
+            product_a(b)
+        differ(2)
+        differ(3)
+        waiting = None
+        for m in range(PACK - 1):
+            ag = ring.tile([P, S], F32, name="ag", bufs=3)
+            fetch("s", ag[:], a_all[:, S * m : S * (m + 2)], n3_t[:])
+            squash(m + 1)
+            keep = kept(m)
+            if waiting is not None:
+                store(*waiting)
+            waiting = (m, slice(0, S), pulled(m, slice(0, S), ag), keep)
+        m = PACK - 1
+        keep = kept(m)
+        store(*waiting)
+        for h in range(2):
+            cols = slice(256 * h, 256 * (h + 1))
+            ag = ring.tile([P, 256], F32, name="ag_half")
+            fetch("s", ag[:], a_all[:, S * m : S * (m + 1)], n3_t[:, 16 * h : 16 * (h + 1)])
+            store(m, cols, pulled(m, cols, ag), keep)

@@ -15,14 +15,19 @@ ACT = mybir.ActivationFunctionType
 
 P = 128
 PACK = 4
-T = 2048
+TOKENS = 2048
 S = 512
+HALF = S // 2
+TILES = 4
 MEMBERS = 4
 BLOCK = 128
-SQUARES_WIDTH = 1024
-SCORES_WIDTH = 528
-ON_SCALAR = ((1, 2), (1, 3), (2, 2), (2, 3))
-FLOPS = 3 * 2 * 512 * 512 * 512
+BLOCKS = S // BLOCK
+LIST_COLUMN = 16
+RUN = 4
+SIGN_COLUMNS = 32
+SQUARES_WIDTH = 2 * S
+SCORES_WIDTH = S + LIST_COLUMN
+FLOPS = 3 * 2 * S * S * S
 
 
 def tile_picked_fkcdpullbgvarbig_none_p_kernel(tc, x_words, x_scales, w1, gn, w2, gs, offs, n1, n2, cand, n3, n4, out):
@@ -42,18 +47,28 @@ def tile_picked_fkcdpullbgvarbig_none_p_kernel(tc, x_words, x_scales, w1, gn, w2
             nc.gpsimd.memset(tile[:, live:width], 0.0)
             return tile
 
-        xs = held.tile([P, T], U8, name="xs", align_bytes=64)
-        nc.vector.memset(xs[:].bitcast(I32), 0)
+        def quantise(words, scales, source):
+            nc.vector.quantize_mx(out=words.bitcast(FP8X4), scales=scales, in_=source)
+
+        def product(acc, lhs_words, lhs_scales, rhs_words, rhs_scales):
+            nc.tensor.matmul_mx(out=acc, lhsT=lhs_words.bitcast(FP8X4), lhsT_scale=lhs_scales,
+                                rhs=rhs_words.bitcast(FP8X4), rhs_scale=rhs_scales, start=True, stop=True)
+
+        def scalar_gather(got, source, offsets):
+            nc.scalar.activation(got, source.indirect(offsets), ACT.Copy)
+
+        x_bytes = held.tile([P, TOKENS], U8, name="x_bytes", align_bytes=64)
+        nc.vector.memset(x_bytes[:].bitcast(I32), 0)
         offs_t = load_list("offs_t", offs)
         cand_t = load_list("cand_t", cand)
         w1_rows = w1.rearrange("(p j) c -> p j c", j=PACK)
-        w1_raw = [held.tile([P, PACK, 256], F32, name="w1_raw%d" % h) for h in range(2)]
-        nc.sync.dma_start(w1_raw[0][:], w1_rows[:, :, 0:256])
+        w1_raw = [held.tile([P, PACK, HALF], F32, name="w1_raw%d" % h) for h in range(2)]
+        nc.sync.dma_start(w1_raw[0][:], w1_rows[:, :, 0:HALF])
         for q in range(4):
-            nc.sync.dma_start(xs[32 * q : 32 * q + 4, :].bitcast(I32), x_scales[0, 4 * q : 4 * q + 4, :].bitcast(I32))
-        xw = held.tile([P, T], U32, name="xw", tag="table", align_bytes=64)
-        nc.sync.dma_start(xw[:].bitcast(I32), x_words[0].rearrange("p n t -> p (n t)").bitcast(I32))
-        nc.sync.dma_start(w1_raw[1][:], w1_rows[:, :, 256:512])
+            nc.sync.dma_start(x_bytes[32 * q : 32 * q + 4, :].bitcast(I32), x_scales[0, 4 * q : 4 * q + 4, :].bitcast(I32))
+        x_table = held.tile([P, TOKENS], U32, name="x_table", tag="table", align_bytes=64)
+        nc.sync.dma_start(x_table[:].bitcast(I32), x_words[0].rearrange("p n t -> p (n t)").bitcast(I32))
+        nc.sync.dma_start(w1_raw[1][:], w1_rows[:, :, HALF:S])
         n1_t = load_list("n1_t", n1)
         gs_t = held.tile([P, PACK], F32, name="gs_t")
         gn_t = held.tile([P, PACK], F32, name="gn_t")
@@ -67,153 +82,139 @@ def tile_picked_fkcdpullbgvarbig_none_p_kernel(tc, x_words, x_scales, w1, gn, w2
         make_identity(nc, ident[:])
         warm = held.tile([P, 1], F32, name="warm")
         nc.scalar.activation(warm[:], ident[:, 0:1], ACT.Abs_reciprocal_sqrt, bias=0.5)
-        sq = [window("sq%d" % t, S, SQUARES_WIDTH) for t in range(PACK)]
+        squares = [window("squares%d" % t, S, SQUARES_WIDTH) for t in range(PACK)]
         y_abs = window("y_abs", PACK * S, (PACK + 1) * S)
-        a_all = window("a_all", PACK * S, (PACK + 1) * S)
-        b_win = [window("b_win%d" % t, S, SCORES_WIDTH) for t in range(PACK)]
+        a_all = window("a_all", TILES * S, (TILES + 1) * S)
+        scores = [window("scores%d" % m, S, SCORES_WIDTH) for m in range(TILES)]
 
-        xq_s = held.tile([P, S], U8, name="xq_s", align_bytes=64)
-        xq_w = held.tile([P, S], U32, name="xq_w", align_bytes=64)
-        xc_s = held.tile([P, S], U8, name="xc_s", align_bytes=64)
-        nc.vector.tensor_copy(xq_s[:], xs[:].indirect(offs_t[:]))
-        nc.vector.tensor_copy(xc_s[:], xs[:].indirect(cand_t[:]))
-        nc.vector.tensor_copy(xq_w[:], xw[:].indirect(offs_t[:]))
+        picked_bytes = held.tile([P, S], U8, name="picked_bytes", align_bytes=64)
+        picked_words = held.tile([P, S], U32, name="picked_words", align_bytes=64)
+        cand_bytes = held.tile([P, S], U8, name="cand_bytes", align_bytes=64)
+        nc.vector.tensor_copy(picked_bytes[:], x_bytes[:].indirect(offs_t[:]))
+        nc.vector.tensor_copy(cand_bytes[:], x_bytes[:].indirect(cand_t[:]))
+        nc.vector.tensor_copy(picked_words[:], x_table[:].indirect(offs_t[:]))
 
-        w1_bf = held.tile([P, PACK * 512], BF16, name="w1_bf", tag="rounded", align_bytes=64)
-        w1_view = w1_bf[:].rearrange("p (t m j) -> p m j t", t=PACK, j=PACK)
-        w1_in = [raw[:].rearrange("p j (m t) -> p m j t", t=PACK) for raw in w1_raw]
-        nc.scalar.copy(w1_view[:, 0:64], w1_in[0])
-        nc.scalar.copy(w1_view[:, 64:96], w1_in[1][:, 0:32])
-        nc.vector.tensor_copy(w1_view[:, 96:128], w1_in[1][:, 32:64])
-        w1_w = held.tile([P, 512], U32, name="w1_w", align_bytes=64)
-        w1_s = held.tile([P, 512], U8, name="w1_s", align_bytes=64)
+        w1_bf = held.tile([P, PACK * S], BF16, name="w1_bf", tag="rounded", align_bytes=64)
+        w1_dealt = w1_bf[:].rearrange("p (t i j) -> p i j t", t=PACK, j=PACK)
+        w1_in = [raw[:].rearrange("p j (i t) -> p i j t", t=PACK) for raw in w1_raw]
+        quarter = P // 4
+        nc.scalar.copy(w1_dealt[:, 0 : 2 * quarter], w1_in[0])
+        nc.scalar.copy(w1_dealt[:, 2 * quarter : 3 * quarter], w1_in[1][:, 0:quarter])
+        nc.vector.tensor_copy(w1_dealt[:, 3 * quarter : P], w1_in[1][:, quarter : 2 * quarter])
+        w1_words = held.tile([P, S], U32, name="w1_words", align_bytes=64)
+        w1_bytes = held.tile([P, S], U8, name="w1_bytes", align_bytes=64)
         y_ps = []
         for t in range(PACK):
             cols = slice(P * t, P * (t + 1))
-            nc.vector.quantize_mx(out=w1_w[:, cols].bitcast(FP8X4), scales=w1_s[:, cols], in_=w1_bf[:, 512 * t : 512 * (t + 1)])
+            quantise(w1_words[:, cols], w1_bytes[:, cols], w1_bf[:, S * t : S * (t + 1)])
             acc = psum.tile([P, S], F32, name="y_ps", tag="acc", bufs=4)
-            nc.tensor.matmul_mx(out=acc[:], lhsT=w1_w[:, cols].bitcast(FP8X4), lhsT_scale=w1_s[:, cols],
-                                rhs=xq_w[:].bitcast(FP8X4), rhs_scale=xq_s[:], start=True, stop=True)
+            product(acc[:], w1_words[:, cols], w1_bytes[:, cols], picked_words[:], picked_bytes[:])
             y_ps.append(acc)
-        xc_w = held.tile([P, S], U32, name="xc_w", tag="rounded", align_bytes=64)
-        nc.vector.tensor_copy(xc_w[:], xw[:].indirect(cand_t[:]))
-        w2_raw = held.tile([P, PACK, 512], F32, name="w2_raw", tag="table", align_bytes=64)
+        cand_words = held.tile([P, S], U32, name="cand_words", tag="rounded", align_bytes=64)
+        nc.vector.tensor_copy(cand_words[:], x_table[:].indirect(cand_t[:]))
+        w2_raw = held.tile([P, PACK, S], F32, name="w2_raw", tag="table", align_bytes=64)
         nc.sync.dma_start(w2_raw[:], w2.rearrange("(p j) c -> p j c", j=PACK))
 
         gs_abs = held.tile([P, PACK], F32, name="gs_abs")
         nc.scalar.activation(gs_abs[:], gs_t[:], ACT.Abs)
-        gs_sign = held.tile([P, BLOCK, PACK], BF16, name="gs_sign")
-        nc.scalar.activation(gs_sign[:], gs_t[:].unsqueeze(1).to_broadcast([P, BLOCK, PACK]), ACT.Sign)
+        gs_sign = held.tile([P, SIGN_COLUMNS, PACK], BF16, name="gs_sign")
+        nc.scalar.activation(gs_sign[:], gs_t[:].unsqueeze(1).to_broadcast([P, SIGN_COLUMNS, PACK]), ACT.Sign)
 
         for t in range(PACK):
-            nc.scalar.activation(sq[t][:, 0:S], y_ps[t][:], ACT.Square)
+            nc.scalar.activation(squares[t][:, 0:S], y_ps[t][:], ACT.Square)
 
-        yn = held.tile([P, PACK, S], F32, name="yn")
-        yg = held.tile([P, PACK, S], F32, name="yg")
-        w2_bf = held.tile([P, PACK * 512], BF16, name="w2_bf", align_bytes=64)
-        w2_w = held.tile([P, 512], U32, name="w2_w", align_bytes=64)
-        w2_s = held.tile([P, 512], U8, name="w2_s", align_bytes=64)
-        z_w = held.tile([P, S], U32, name="z_w", align_bytes=64)
-        z_s = held.tile([P, S], U8, name="z_s", align_bytes=64)
-        top_bf = held.tile([P, PACK * S], BF16, name="top_bf", tag="planes", align_bytes=64)
-        z2_bf = held.tile([P, PACK * S], BF16, name="z2_bf", tag="woven", align_bytes=64)
-        z2_w = held.tile([P, S], U32, name="z2_w", align_bytes=64)
-        z2_s = held.tile([P, S], U8, name="z2_s", align_bytes=64)
-        db = held.tile([P, PACK, S], F32, name="db")
+        y_gain = held.tile([P, PACK, S], F32, name="y_gain")
+        y_other = held.tile([P, PACK, S], F32, name="y_other")
+        w2_bf = held.tile([P, PACK * S], BF16, name="w2_bf", align_bytes=64)
+        w2_words = held.tile([P, S], U32, name="w2_words", align_bytes=64)
+        w2_bytes = held.tile([P, S], U8, name="w2_bytes", align_bytes=64)
+        z_words = held.tile([P, S], U32, name="z_words", align_bytes=64)
+        z_bytes = held.tile([P, S], U8, name="z_bytes", align_bytes=64)
+        larger_bf = held.tile([P, PACK * S], BF16, name="larger_bf", tag="woven", align_bytes=64)
+        z2_bf = held.tile([P, PACK * S], BF16, name="z2_bf", tag="stage", align_bytes=64)
+        z2_words = held.tile([P, S], U32, name="z2_words", align_bytes=64)
+        z2_bytes = held.tile([P, S], U8, name="z2_bytes", align_bytes=64)
+        b_diff = held.tile([P, TILES, S], F32, name="b_diff")
         sums = {}
 
-        def members(b, t, g):
-            offsets = n1_t[:, 32 * b : 32 * (b + 1)]
+        def members(b, t, got):
+            offsets = n1_t[:, b * MEMBERS * BLOCK // LIST_COLUMN : (b + 1) * MEMBERS * BLOCK // LIST_COLUMN]
             if b not in sums:
                 sums[b] = psum.tile([P, PACK, P], F32, name="sums", tag="sums")
-            if (b, t) in ON_SCALAR:
-                nc.scalar.activation(g, sq[t][:].indirect(offsets), ACT.Copy)
-                member = g.rearrange("p (j u) -> p u j", u=MEMBERS)
+            if b in (1, 2) and t >= 2:
+                scalar_gather(got, squares[t][:], offsets)
+                member = got.rearrange("p (j u) -> p u j", u=MEMBERS)
             else:
-                member = g.rearrange("p (u j) -> p u j", u=MEMBERS)
-                nc.vector.tensor_copy(member.rearrange("p u j -> p j u"), sq[t][:].indirect(offsets))
+                member = got.rearrange("p (u j) -> p u j", u=MEMBERS)
+                nc.vector.tensor_copy(member.rearrange("p u j -> p j u"), squares[t][:].indirect(offsets))
             for u in range(MEMBERS):
                 nc.tensor.matmul(sums[b][:, t, :], member[:, u, :], ident[:], start=(u == 0), stop=(u == MEMBERS - 1), is_transpose=True)
 
         def early_members(b, t):
-            g = ring.tile([P, MEMBERS * BLOCK], F32, name="early", bufs=8)
-            members(b, t, g[:])
+            got = ring.tile([P, MEMBERS * BLOCK], F32, name="early", bufs=2 * PACK)
+            members(b, t, got[:])
 
-        def inverse_root(b, r_flat):
-            r_t = r_flat.rearrange("p (t i) -> p t i", t=PACK)
-            nc.scalar.activation(r_t, sums[b][:], ACT.Abs_reciprocal_sqrt, bias=0.5)
-            r = psum.tile([P, PACK, P], F32, name="r", tag="r")
+        def inverse_root(b, room):
+            turned = room.rearrange("p (t i) -> p t i", t=PACK)
+            nc.scalar.activation(turned, sums[b][:], ACT.Abs_reciprocal_sqrt, bias=0.5)
+            root = psum.tile([P, PACK, P], F32, name="root", tag="root")
             for t in range(PACK):
-                nc.tensor.transpose(r[:, t, :], r_t[:, t, :], ident[:])
-            return r
+                nc.tensor.transpose(root[:, t, :], turned[:, t, :], ident[:])
+            return root
 
-        def make_z(b, r):
-            cols = slice(BLOCK * b, BLOCK * (b + 1))
-            wide = slice(PACK * BLOCK * b, PACK * BLOCK * (b + 1))
-            nc.vector.tensor_tensor(z_bf[:, wide].rearrange("p (c i t) -> p c t i", i=4, t=PACK),
-                                    r[:].rearrange("p t (c i) -> p c t i", i=4),
-                                    yn[:, :, cols].rearrange("p t (c i) -> p c t i", i=4), ALU.mult)
+        def woven(ap):
+            return ap.rearrange("p (c i t) -> p c t i", i=RUN, t=PACK)
+
+        def by_runs(ap):
+            return ap.rearrange("p t (c i) -> p c t i", i=RUN)
+
+        def make_z(b, root):
+            nc.vector.tensor_tensor(woven(z_bf[:, PACK * BLOCK * b : PACK * BLOCK * (b + 1)]), by_runs(root[:]),
+                                    by_runs(y_gain[:, :, BLOCK * b : BLOCK * (b + 1)]), ALU.mult)
 
         def quantise_z(b):
             cols = slice(BLOCK * b, BLOCK * (b + 1))
-            wide = slice(PACK * BLOCK * b, PACK * BLOCK * (b + 1))
-            nc.vector.quantize_mx(out=z_w[:, cols].bitcast(FP8X4), scales=z_s[:, cols], in_=z_bf[:, wide])
-
-        def evac(eng, to, ps):
-            if eng == "v":
-                nc.vector.tensor_copy(to, ps)
-            else:
-                nc.scalar.copy(to, ps)
-
-        def fetch(eng, got, win, offsets):
-            if eng == "v":
-                nc.vector.tensor_copy(got, win.indirect(offsets))
-            else:
-                nc.scalar.activation(got, win.indirect(offsets), ACT.Copy)
+            quantise(z_words[:, cols], z_bytes[:, cols], z_bf[:, PACK * BLOCK * b : PACK * BLOCK * (b + 1)])
 
         def product_b(m):
-            cols = slice(P * m, P * (m + 1))
+            rows = slice(P * m, P * (m + 1))
             acc = psum.tile([P, S], F32, name="b_ps", tag="acc", bufs=4)
-            nc.tensor.matmul_mx(out=acc[:], lhsT=xc_w[:, cols].bitcast(FP8X4), lhsT_scale=xc_s[:, cols],
-                                rhs=z2_w[:].bitcast(FP8X4), rhs_scale=z2_s[:], start=True, stop=True)
+            product(acc[:], cand_words[:, rows], cand_bytes[:, rows], z2_words[:], z2_bytes[:])
             return acc
 
         def product_a(b):
             cols = slice(BLOCK * b, BLOCK * (b + 1))
-            acc = psum.tile([P, PACK, BLOCK], F32, name="a_ps", tag="sums") if b < 2 else psum.tile([P, PACK, BLOCK], F32, name="a_ps", tag="acc", bufs=4)
-            for m in range(PACK):
+            if b < 2:
+                acc = psum.tile([P, TILES, BLOCK], F32, name="a_ps", tag="sums")
+            else:
+                acc = psum.tile([P, TILES, BLOCK], F32, name="a_ps", tag="acc", bufs=4)
+            for m in range(TILES):
                 rows = slice(P * m, P * (m + 1))
-                nc.tensor.matmul_mx(out=acc[:, m, :], lhsT=w2_w[:, rows].bitcast(FP8X4), lhsT_scale=w2_s[:, rows],
-                                    rhs=z_w[:, cols].bitcast(FP8X4), rhs_scale=z_s[:, cols], start=True, stop=True)
-            evac("vvvv"[b], a_all[:, 0 : PACK * S].rearrange("p (m j) -> p m j", m=PACK)[:, :, cols], acc[:])
+                product(acc[:, m, :], w2_words[:, rows], w2_bytes[:, rows], z_words[:, cols], z_bytes[:, cols])
+            nc.vector.tensor_copy(a_all[:, 0 : TILES * S].rearrange("p (m j) -> p m j", m=TILES)[:, :, cols], acc[:])
 
-        bg = [ring.tile([P, S], F32, name="bg%d" % m, bufs=1) for m in range(PACK)]
+        b_other = [held.tile([P, S], F32, name="b_other%d" % m) for m in range(TILES)]
 
         def copy_b(m):
-            nc.scalar.copy(b_win[m][:, 0:S], b_ps[m][:])
+            nc.scalar.copy(scores[m][:, 0:S], b_ps[m][:])
 
-        def fetch_b(m):
-            fetch("ssss"[m], bg[m][:], b_win[m][:], n4_t[:])
+        def gather_b(m):
+            scalar_gather(b_other[m][:], scores[m][:], n4_t[:])
 
-        def differ(m):
-            nc.vector.tensor_tensor(db[:, m, :], bg[m][:], b_win[m][:, 0:S], ALU.subtract)
+        def subtract_b(m):
+            nc.vector.tensor_tensor(b_diff[:, m, :], b_other[m][:], scores[m][:, 0:S], ALU.subtract)
 
-        def squash(m):
-            nc.scalar.activation(gates[:, m, :], db[:, m, :], ACT.Sigmoid, scale=0.0625)
+        def make_gate(m):
+            nc.scalar.activation(gates[:, m, :], b_diff[:, m, :], ACT.Sigmoid, scale=0.0625)
 
-        def kept(m):
-            keep = ring.tile([P, S], F32, name="keep", bufs=4)
-            nc.vector.scalar_tensor_tensor(keep[:], gates[:, m, :], 1.0, a_all[:, S * m : S * (m + 1)], ALU.subtract, ALU.mult)
-            return keep
+        def own_term(m):
+            own = ring.tile([P, S], F32, name="own", bufs=TILES)
+            nc.vector.scalar_tensor_tensor(own[:], gates[:, m, :], 1.0, a_all[:, S * m : S * (m + 1)], ALU.subtract, ALU.mult)
+            return own
 
-        def pulled(m, cols, ag):
-            pull = ring.tile([P, cols.stop - cols.start], F32, name="pull", bufs=3)
-            nc.vector.tensor_tensor(pull[:], ag[:], gates[:, m, cols], ALU.mult)
-            return pull
-
-        def store(m, cols, pull, keep):
-            res = ring.tile([P, cols.stop - cols.start], F32, name="res", bufs=5)
-            nc.vector.tensor_tensor(res[:], pull[:], keep[:, cols], ALU.subtract)
+        def store(m, cols, pulled):
+            res = ring.tile([P, cols.stop - cols.start], F32, name="res", bufs=len(pieces))
+            nc.vector.tensor_tensor(res[:], pulled[:], own[m][:, cols], ALU.subtract)
             nc.sync.dma_start(out[P * m : P * (m + 1), cols], res[:])
 
         for t in range(PACK):
@@ -222,80 +223,82 @@ def tile_picked_fkcdpullbgvarbig_none_p_kernel(tc, x_words, x_scales, w1, gn, w2
             if t < PACK:
                 nc.scalar.activation(y_abs[:, S * t : S * (t + 1)], y_ps[t][:], ACT.Copy, scale=gs_abs[:, t : t + 1])
             if t > 0:
-                fetch("s", yg[:, t - 1, :], y_abs[:, S * (t - 1) : S * (t + 1)], n2_t[:])
-        root0 = held.tile([P, S], F32, name="root0")
-        r0 = inverse_root(0, root0[:])
-        nc.vector.tensor_tensor(top_bf[:].rearrange("p (c i t) -> p c t i", i=4, t=PACK),
-                                yg[:].rearrange("p t (c i) -> p c t i", i=4),
-                                y_abs[:, 0 : PACK * S].rearrange("p (t c i) -> p c t i", t=PACK, i=4), ALU.max)
+                scalar_gather(y_other[:, t - 1, :], y_abs[:, S * (t - 1) : S * (t + 1)], n2_t[:])
+        turned0 = held.tile([P, PACK * P], F32, name="turned0")
+        root0 = inverse_root(0, turned0[:])
+        nc.vector.tensor_tensor(woven(larger_bf[:]), by_runs(y_other[:]),
+                                by_runs(y_abs[:, 0 : PACK * S].rearrange("p (t c) -> p t c", t=PACK)), ALU.max)
         for t in range(PACK):
             early_members(1, t)
         for t in range(PACK):
-            nc.scalar.activation(yn[:, t, :], y_ps[t][:], ACT.Copy, scale=gn_t[:, t : t + 1])
-        nc.vector.tensor_tensor(z2_bf[:].rearrange("p (b w) -> p b w", b=4), top_bf[:].rearrange("p (b w) -> p b w", b=4),
-                                gs_sign[:].rearrange("p c t -> p (c t)").unsqueeze(1).to_broadcast([P, 4, PACK * BLOCK]), ALU.mult)
-        for h in range(4):
-            cols = slice(P * h, P * (h + 1))
-            nc.vector.tensor_copy(w2_bf[:, PACK * P * h : PACK * P * (h + 1)].rearrange("p (c i j) -> p c j i", i=4, j=PACK),
-                                  w2_raw[:, :, cols].rearrange("p j (c i) -> p c j i", i=4))
-        nc.vector.quantize_mx(out=z2_w[:].bitcast(FP8X4), scales=z2_s[:], in_=z2_bf[:])
-        b_ps = [product_b(m) for m in range(PACK)]
-        z_bf = held.tile([P, PACK * S], BF16, name="z_bf", tag="planes", align_bytes=64)
-        late = held.tile([P, 3, PACK, MEMBERS * BLOCK], F32, name="late", tag="woven", align_bytes=64)
+            nc.scalar.activation(y_gain[:, t, :], y_ps[t][:], ACT.Copy, scale=gn_t[:, t : t + 1])
+        repeats = S // SIGN_COLUMNS
+        nc.vector.tensor_tensor(z2_bf[:].rearrange("p (r w) -> p r w", r=repeats), larger_bf[:].rearrange("p (r w) -> p r w", r=repeats),
+                                gs_sign[:].rearrange("p c t -> p (c t)").unsqueeze(1).to_broadcast([P, repeats, PACK * SIGN_COLUMNS]), ALU.mult)
+        for m in range(TILES):
+            nc.vector.tensor_copy(w2_bf[:, PACK * P * m : PACK * P * (m + 1)].rearrange("p (c i j) -> p c j i", i=RUN, j=PACK),
+                                  w2_raw[:, :, P * m : P * (m + 1)].rearrange("p j (c i) -> p c j i", i=RUN))
+        quantise(z2_words[:], z2_bytes[:], z2_bf[:])
+        b_ps = [product_b(m) for m in range(TILES)]
+
+        z_bf = held.tile([P, PACK * S], BF16, name="z_bf", tag="woven", align_bytes=64)
+        late = held.tile([P, 2 * PACK + BLOCKS - 1, MEMBERS * BLOCK], F32, name="late", tag="stage", align_bytes=64)
 
         def late_members(b, t):
-            members(b, t, late[:, b - 2, t, :])
+            members(b, t, late[:, PACK * (b - 2) + t, :])
 
-        r1 = inverse_root(1, late[:, 2, 1, :])
+        def late_root(b):
+            return inverse_root(b, late[:, 2 * PACK + b - 1, :])
+
+        root1 = late_root(1)
         late_members(2, 2)
         late_members(2, 3)
-        make_z(0, r0)
+        make_z(0, root0)
         late_members(2, 0)
         quantise_z(0)
         late_members(2, 1)
-        nc.vector.quantize_mx(out=w2_w[:].bitcast(FP8X4), scales=w2_s[:], in_=w2_bf[:])
-        make_z(1, r1)
+        quantise(w2_words[:], w2_bytes[:], w2_bf[:])
+        make_z(1, root1)
         late_members(3, 0)
         quantise_z(1)
         for t in range(1, PACK):
             late_members(3, t)
         copy_b(0)
         copy_b(1)
-        fetch_b(0)
+        gather_b(0)
         copy_b(2)
         copy_b(3)
-        fetch_b(1)
-        r2 = inverse_root(2, late[:, 2, 2, :])
-        fetch_b(2)
-        r3 = inverse_root(3, late[:, 2, 3, :])
-        fetch_b(3)
-        differ(0)
-        make_z(2, r2)
-        differ(1)
+        gather_b(1)
+        root2 = late_root(2)
+        gather_b(2)
+        root3 = late_root(3)
+        gather_b(3)
+        subtract_b(0)
+        make_z(2, root2)
+        subtract_b(1)
         quantise_z(2)
-        make_z(3, r3)
+        make_z(3, root3)
         product_a(0)
         quantise_z(3)
-        gates = held.tile([P, PACK, S], F32, name="gates", tag="woven", align_bytes=64)
-        squash(0)
-        for b in range(1, 4):
+
+        gates = held.tile([P, TILES, S], F32, name="gates", tag="stage", align_bytes=64)
+        make_gate(0)
+        for b in range(1, BLOCKS):
             product_a(b)
-        differ(2)
-        differ(3)
+        subtract_b(2)
+        subtract_b(3)
+        for m in range(1, TILES):
+            make_gate(m)
+        own = [own_term(m) for m in range(TILES)]
+        pieces = [(m, slice(0, S)) for m in range(TILES - 1)] + [(TILES - 1, slice(0, HALF)), (TILES - 1, slice(HALF, S))]
         waiting = None
-        for m in range(PACK - 1):
-            ag = ring.tile([P, S], F32, name="ag", bufs=3)
-            fetch("s", ag[:], a_all[:, S * m : S * (m + 2)], n3_t[:])
-            squash(m + 1)
-            keep = kept(m)
+        for m, cols in pieces:
+            width = cols.stop - cols.start
+            a_other = ring.tile([P, width], F32, name="a_other", bufs=len(pieces))
+            scalar_gather(a_other[:], a_all[:, S * m : S * m + 2 * width], n3_t[:, cols.start // LIST_COLUMN : cols.stop // LIST_COLUMN])
+            pulled = ring.tile([P, width], F32, name="pulled", bufs=3)
+            nc.vector.tensor_tensor(pulled[:], a_other[:], gates[:, m, cols], ALU.mult)
             if waiting is not None:
                 store(*waiting)
-            waiting = (m, slice(0, S), pulled(m, slice(0, S), ag), keep)
-        m = PACK - 1
-        keep = kept(m)
+            waiting = (m, cols, pulled)
         store(*waiting)
-        for h in range(2):
-            cols = slice(256 * h, 256 * (h + 1))
-            ag = ring.tile([P, 256], F32, name="ag_half")
-            fetch("s", ag[:], a_all[:, S * m : S * (m + 1)], n3_t[:, 16 * h : 16 * (h + 1)])
-            store(m, cols, pulled(m, cols, ag), keep)

from contextlib import ExitStack

import concourse.mybir as mybir
from concourse.masks import make_identity

F32 = mybir.dt.float32
BF16 = mybir.dt.bfloat16
I32 = mybir.dt.int32
U32 = mybir.dt.uint32
U16 = mybir.dt.uint16
U8 = mybir.dt.uint8
FP8X4 = mybir.dt.float8_e4m3fn_x4
ALU = mybir.AluOpType
ACT = mybir.ActivationFunctionType

P = 128
PACK = 4
TOKENS = 2048
S = 512
HALF = S // 2
TILES = 4
MEMBERS = 4
BLOCK = 128
BLOCKS = S // BLOCK
LIST_COLUMN = 16
RUN = 4
SIGN_COLUMNS = 32
SQUARES_WIDTH = 2 * S
SCORES_WIDTH = S + LIST_COLUMN
FLOPS = 3 * 2 * S * S * S


def tile_picked_fkcdpullbgvarbig_none_p_kernel(tc, x_words, x_scales, w1, gn, w2, gs, offs, n1, n2, cand, n3, n4, out):
    nc = tc.nc
    with ExitStack() as ctx:
        held = ctx.enter_context(tc.tile_pool(name="held", bufs=1))
        ring = ctx.enter_context(tc.tile_pool(name="ring", bufs=2))
        psum = ctx.enter_context(tc.psum_pool(name="psum", bufs=2))

        def load_list(name, dram):
            tile = held.tile(list(dram.shape), U16, name=name)
            nc.sync.dma_start(tile[:], dram)
            return tile

        def window(name, live, width):
            tile = held.tile([P, width], F32, name=name)
            nc.gpsimd.memset(tile[:, live:width], 0.0)
            return tile

        def quantise(words, scales, source):
            nc.vector.quantize_mx(out=words.bitcast(FP8X4), scales=scales, in_=source)

        def product(acc, lhs_words, lhs_scales, rhs_words, rhs_scales):
            nc.tensor.matmul_mx(out=acc, lhsT=lhs_words.bitcast(FP8X4), lhsT_scale=lhs_scales,
                                rhs=rhs_words.bitcast(FP8X4), rhs_scale=rhs_scales, start=True, stop=True)

        def scalar_gather(got, source, offsets):
            nc.scalar.activation(got, source.indirect(offsets), ACT.Copy)

        x_bytes = held.tile([P, TOKENS], U8, name="x_bytes", align_bytes=64)
        nc.vector.memset(x_bytes[:].bitcast(I32), 0)
        offs_t = load_list("offs_t", offs)
        cand_t = load_list("cand_t", cand)
        w1_rows = w1.rearrange("(p j) c -> p j c", j=PACK)
        w1_raw = [held.tile([P, PACK, HALF], F32, name="w1_raw%d" % h) for h in range(2)]
        nc.sync.dma_start(w1_raw[0][:], w1_rows[:, :, 0:HALF])
        for q in range(4):
            nc.sync.dma_start(x_bytes[32 * q : 32 * q + 4, :].bitcast(I32), x_scales[0, 4 * q : 4 * q + 4, :].bitcast(I32))
        x_table = held.tile([P, TOKENS], U32, name="x_table", tag="table", align_bytes=64)
        nc.sync.dma_start(x_table[:].bitcast(I32), x_words[0].rearrange("p n t -> p (n t)").bitcast(I32))
        nc.sync.dma_start(w1_raw[1][:], w1_rows[:, :, HALF:S])
        n1_t = load_list("n1_t", n1)
        gs_t = held.tile([P, PACK], F32, name="gs_t")
        gn_t = held.tile([P, PACK], F32, name="gn_t")
        nc.sync.dma_start(gs_t[:], gs.rearrange("(p t) o -> p (t o)", t=PACK))
        n2_t = load_list("n2_t", n2)
        nc.sync.dma_start(gn_t[:], gn.rearrange("(p t) o -> p (t o)", t=PACK))
        n4_t = load_list("n4_t", n4)
        n3_t = load_list("n3_t", n3)

        ident = held.tile([P, P], F32, name="ident")
        make_identity(nc, ident[:])
        warm = held.tile([P, 1], F32, name="warm")
        nc.scalar.activation(warm[:], ident[:, 0:1], ACT.Abs_reciprocal_sqrt, bias=0.5)
        squares = [window("squares%d" % t, S, SQUARES_WIDTH) for t in range(PACK)]
        y_abs = window("y_abs", PACK * S, (PACK + 1) * S)
        a_all = window("a_all", TILES * S, (TILES + 1) * S)
        scores = [window("scores%d" % m, S, SCORES_WIDTH) for m in range(TILES)]

        picked_bytes = held.tile([P, S], U8, name="picked_bytes", align_bytes=64)
        picked_words = held.tile([P, S], U32, name="picked_words", align_bytes=64)
        cand_bytes = held.tile([P, S], U8, name="cand_bytes", align_bytes=64)
        nc.vector.tensor_copy(picked_bytes[:], x_bytes[:].indirect(offs_t[:]))
        nc.vector.tensor_copy(cand_bytes[:], x_bytes[:].indirect(cand_t[:]))
        nc.vector.tensor_copy(picked_words[:], x_table[:].indirect(offs_t[:]))

        w1_bf = held.tile([P, PACK * S], BF16, name="w1_bf", tag="rounded", align_bytes=64)
        w1_dealt = w1_bf[:].rearrange("p (t i j) -> p i j t", t=PACK, j=PACK)
        w1_in = [raw[:].rearrange("p j (i t) -> p i j t", t=PACK) for raw in w1_raw]
        quarter = P // 4
        nc.scalar.copy(w1_dealt[:, 0 : 2 * quarter], w1_in[0])
        nc.scalar.copy(w1_dealt[:, 2 * quarter : 3 * quarter], w1_in[1][:, 0:quarter])
        nc.vector.tensor_copy(w1_dealt[:, 3 * quarter : P], w1_in[1][:, quarter : 2 * quarter])
        w1_words = held.tile([P, S], U32, name="w1_words", align_bytes=64)
        w1_bytes = held.tile([P, S], U8, name="w1_bytes", align_bytes=64)
        y_ps = []
        for t in range(PACK):
            cols = slice(P * t, P * (t + 1))
            quantise(w1_words[:, cols], w1_bytes[:, cols], w1_bf[:, S * t : S * (t + 1)])
            acc = psum.tile([P, S], F32, name="y_ps", tag="acc", bufs=4)
            product(acc[:], w1_words[:, cols], w1_bytes[:, cols], picked_words[:], picked_bytes[:])
            y_ps.append(acc)
        cand_words = held.tile([P, S], U32, name="cand_words", tag="rounded", align_bytes=64)
        nc.vector.tensor_copy(cand_words[:], x_table[:].indirect(cand_t[:]))
        w2_raw = held.tile([P, PACK, S], F32, name="w2_raw", tag="table", align_bytes=64)
        nc.sync.dma_start(w2_raw[:], w2.rearrange("(p j) c -> p j c", j=PACK))

        gs_abs = held.tile([P, PACK], F32, name="gs_abs")
        nc.scalar.activation(gs_abs[:], gs_t[:], ACT.Abs)
        gs_sign = held.tile([P, SIGN_COLUMNS, PACK], BF16, name="gs_sign")
        nc.scalar.activation(gs_sign[:], gs_t[:].unsqueeze(1).to_broadcast([P, SIGN_COLUMNS, PACK]), ACT.Sign)

        for t in range(PACK):
            nc.scalar.activation(squares[t][:, 0:S], y_ps[t][:], ACT.Square)

        y_gain = held.tile([P, PACK, S], F32, name="y_gain")
        y_other = held.tile([P, PACK, S], F32, name="y_other")
        w2_bf = held.tile([P, PACK * S], BF16, name="w2_bf", align_bytes=64)
        w2_words = held.tile([P, S], U32, name="w2_words", align_bytes=64)
        w2_bytes = held.tile([P, S], U8, name="w2_bytes", align_bytes=64)
        z_words = held.tile([P, S], U32, name="z_words", align_bytes=64)
        z_bytes = held.tile([P, S], U8, name="z_bytes", align_bytes=64)
        larger_bf = held.tile([P, PACK * S], BF16, name="larger_bf", tag="woven", align_bytes=64)
        z2_bf = held.tile([P, PACK * S], BF16, name="z2_bf", tag="stage", align_bytes=64)
        z2_words = held.tile([P, S], U32, name="z2_words", align_bytes=64)
        z2_bytes = held.tile([P, S], U8, name="z2_bytes", align_bytes=64)
        b_diff = held.tile([P, TILES, S], F32, name="b_diff")
        sums = {}

        def members(b, t, got):
            offsets = n1_t[:, b * MEMBERS * BLOCK // LIST_COLUMN : (b + 1) * MEMBERS * BLOCK // LIST_COLUMN]
            if b not in sums:
                sums[b] = psum.tile([P, PACK, P], F32, name="sums", tag="sums")
            if b in (1, 2) and t >= 2:
                scalar_gather(got, squares[t][:], offsets)
                member = got.rearrange("p (j u) -> p u j", u=MEMBERS)
            else:
                member = got.rearrange("p (u j) -> p u j", u=MEMBERS)
                nc.vector.tensor_copy(member.rearrange("p u j -> p j u"), squares[t][:].indirect(offsets))
            for u in range(MEMBERS):
                nc.tensor.matmul(sums[b][:, t, :], member[:, u, :], ident[:], start=(u == 0), stop=(u == MEMBERS - 1), is_transpose=True)

        def early_members(b, t):
            got = ring.tile([P, MEMBERS * BLOCK], F32, name="early", bufs=2 * PACK)
            members(b, t, got[:])

        def inverse_root(b, room):
            turned = room.rearrange("p (t i) -> p t i", t=PACK)
            nc.scalar.activation(turned, sums[b][:], ACT.Abs_reciprocal_sqrt, bias=0.5)
            root = psum.tile([P, PACK, P], F32, name="root", tag="root")
            for t in range(PACK):
                nc.tensor.transpose(root[:, t, :], turned[:, t, :], ident[:])
            return root

        def woven(ap):
            return ap.rearrange("p (c i t) -> p c t i", i=RUN, t=PACK)

        def by_runs(ap):
            return ap.rearrange("p t (c i) -> p c t i", i=RUN)

        def make_z(b, root):
            nc.vector.tensor_tensor(woven(z_bf[:, PACK * BLOCK * b : PACK * BLOCK * (b + 1)]), by_runs(root[:]),
                                    by_runs(y_gain[:, :, BLOCK * b : BLOCK * (b + 1)]), ALU.mult)

        def quantise_z(b):
            cols = slice(BLOCK * b, BLOCK * (b + 1))
            quantise(z_words[:, cols], z_bytes[:, cols], z_bf[:, PACK * BLOCK * b : PACK * BLOCK * (b + 1)])

        def product_b(m):
            rows = slice(P * m, P * (m + 1))
            acc = psum.tile([P, S], F32, name="b_ps", tag="acc", bufs=4)
            product(acc[:], cand_words[:, rows], cand_bytes[:, rows], z2_words[:], z2_bytes[:])
            return acc

        def product_a(b):
            cols = slice(BLOCK * b, BLOCK * (b + 1))
            if b < 2:
                acc = psum.tile([P, TILES, BLOCK], F32, name="a_ps", tag="sums")
            else:
                acc = psum.tile([P, TILES, BLOCK], F32, name="a_ps", tag="acc", bufs=4)
            for m in range(TILES):
                rows = slice(P * m, P * (m + 1))
                product(acc[:, m, :], w2_words[:, rows], w2_bytes[:, rows], z_words[:, cols], z_bytes[:, cols])
            nc.vector.tensor_copy(a_all[:, 0 : TILES * S].rearrange("p (m j) -> p m j", m=TILES)[:, :, cols], acc[:])

        b_other = [held.tile([P, S], F32, name="b_other%d" % m) for m in range(TILES)]

        def copy_b(m):
            nc.scalar.copy(scores[m][:, 0:S], b_ps[m][:])

        def gather_b(m):
            scalar_gather(b_other[m][:], scores[m][:], n4_t[:])

        def subtract_b(m):
            nc.vector.tensor_tensor(b_diff[:, m, :], b_other[m][:], scores[m][:, 0:S], ALU.subtract)

        def make_gate(m):
            nc.scalar.activation(gates[:, m, :], b_diff[:, m, :], ACT.Sigmoid, scale=0.0625)

        def own_term(m):
            own = ring.tile([P, S], F32, name="own", bufs=TILES)
            nc.vector.scalar_tensor_tensor(own[:], gates[:, m, :], 1.0, a_all[:, S * m : S * (m + 1)], ALU.subtract, ALU.mult)
            return own

        def store(m, cols, pulled):
            res = ring.tile([P, cols.stop - cols.start], F32, name="res", bufs=len(pieces))
            nc.vector.tensor_tensor(res[:], pulled[:], own[m][:, cols], ALU.subtract)
            nc.sync.dma_start(out[P * m : P * (m + 1), cols], res[:])

        for t in range(PACK):
            early_members(0, t)
        for t in range(PACK + 1):
            if t < PACK:
                nc.scalar.activation(y_abs[:, S * t : S * (t + 1)], y_ps[t][:], ACT.Copy, scale=gs_abs[:, t : t + 1])
            if t > 0:
                scalar_gather(y_other[:, t - 1, :], y_abs[:, S * (t - 1) : S * (t + 1)], n2_t[:])
        turned0 = held.tile([P, PACK * P], F32, name="turned0")
        root0 = inverse_root(0, turned0[:])
        nc.vector.tensor_tensor(woven(larger_bf[:]), by_runs(y_other[:]),
                                by_runs(y_abs[:, 0 : PACK * S].rearrange("p (t c) -> p t c", t=PACK)), ALU.max)
        for t in range(PACK):
            early_members(1, t)
        for t in range(PACK):
            nc.scalar.activation(y_gain[:, t, :], y_ps[t][:], ACT.Copy, scale=gn_t[:, t : t + 1])
        repeats = S // SIGN_COLUMNS
        nc.vector.tensor_tensor(z2_bf[:].rearrange("p (r w) -> p r w", r=repeats), larger_bf[:].rearrange("p (r w) -> p r w", r=repeats),
                                gs_sign[:].rearrange("p c t -> p (c t)").unsqueeze(1).to_broadcast([P, repeats, PACK * SIGN_COLUMNS]), ALU.mult)
        for m in range(TILES):
            nc.vector.tensor_copy(w2_bf[:, PACK * P * m : PACK * P * (m + 1)].rearrange("p (c i j) -> p c j i", i=RUN, j=PACK),
                                  w2_raw[:, :, P * m : P * (m + 1)].rearrange("p j (c i) -> p c j i", i=RUN))
        quantise(z2_words[:], z2_bytes[:], z2_bf[:])
        b_ps = [product_b(m) for m in range(TILES)]

        z_bf = held.tile([P, PACK * S], BF16, name="z_bf", tag="woven", align_bytes=64)
        late = held.tile([P, 2 * PACK + BLOCKS - 1, MEMBERS * BLOCK], F32, name="late", tag="stage", align_bytes=64)

        def late_members(b, t):
            members(b, t, late[:, PACK * (b - 2) + t, :])

        def late_root(b):
            return inverse_root(b, late[:, 2 * PACK + b - 1, :])

        root1 = late_root(1)
        late_members(2, 2)
        late_members(2, 3)
        make_z(0, root0)
        late_members(2, 0)
        quantise_z(0)
        late_members(2, 1)
        quantise(w2_words[:], w2_bytes[:], w2_bf[:])
        make_z(1, root1)
        late_members(3, 0)
        quantise_z(1)
        for t in range(1, PACK):
            late_members(3, t)
        copy_b(0)
        copy_b(1)
        gather_b(0)
        copy_b(2)
        copy_b(3)
        gather_b(1)
        root2 = late_root(2)
        gather_b(2)
        root3 = late_root(3)
        gather_b(3)
        subtract_b(0)
        make_z(2, root2)
        subtract_b(1)
        quantise_z(2)
        make_z(3, root3)
        product_a(0)
        quantise_z(3)

        gates = held.tile([P, TILES, S], F32, name="gates", tag="stage", align_bytes=64)
        make_gate(0)
        for b in range(1, BLOCKS):
            product_a(b)
        subtract_b(2)
        subtract_b(3)
        for m in range(1, TILES):
            make_gate(m)
        own = [own_term(m) for m in range(TILES)]
        pieces = [(m, slice(0, S)) for m in range(TILES - 1)] + [(TILES - 1, slice(0, HALF)), (TILES - 1, slice(HALF, S))]
        waiting = None
        for m, cols in pieces:
            width = cols.stop - cols.start
            a_other = ring.tile([P, width], F32, name="a_other", bufs=len(pieces))
            scalar_gather(a_other[:], a_all[:, S * m : S * m + 2 * width], n3_t[:, cols.start // LIST_COLUMN : cols.stop // LIST_COLUMN])
            pulled = ring.tile([P, width], F32, name="pulled", bufs=3)
            nc.vector.tensor_tensor(pulled[:], a_other[:], gates[:, m, cols], ALU.mult)
            if waiting is not None:
                store(*waiting)
            waiting = (m, cols, pulled)
        store(*waiting)
